import numpy as np, ml_dtypes
CORES = [45,53,77,117,47,55,79,119]
N = 8
TK = 64
def gelu(z): return 0.5 * z * (1.0 + np.tanh(0.7978845608028654 * (z + 0.044715 * z ** 3)))
def setup_inputs(rng):
    return {"x": rng.standard_normal((N, 128, TK), dtype=np.float32).astype(ml_dtypes.bfloat16), "w1": (rng.standard_normal((N, 128, 128), dtype=np.float32) / 8).astype(ml_dtypes.bfloat16), "w2": (rng.standard_normal((N, 128, 128), dtype=np.float32) / 8).astype(ml_dtypes.bfloat16)}
def setup_inputs_big(rng):
    d = setup_inputs(rng)
    for k in ("x",): d[k] = (d[k].astype(np.float32) * 1024.0).astype(d[k].dtype)
    return d
def setup_inputs_small(rng):
    d = setup_inputs(rng)
    for k in ("x",): d[k] = (d[k].astype(np.float32) * (1 / 1024.0)).astype(d[k].dtype)
    return d
def setup_inputs_apart(rng):
    d = setup_inputs(rng)
    f = (10.0 ** rng.permutation(np.linspace(-1.5, 1.5, N))).astype(np.float32).reshape(N, 1, 1)
    for k in ("x",): d[k] = (d[k].astype(np.float32) * f).astype(d[k].dtype)
    return d
def reference(x, w1, w2):
    X, W1, W2 = x.astype(np.float64), w1.astype(np.float64), w2.astype(np.float64)
    y = np.zeros((N, 128, TK))
    for r in range(N):
        for j in range(N):
            y[r] += W2[j].T @ (gelu(W1[j].T @ X[r]))
    return {"y": y.astype(ml_dtypes.bfloat16)}

@@ -1,0 +1,186 @@
+from concourse.bass import DstId, RemoteDMATransfer
+from concourse.mybir import AluOpType, ActivationFunctionType
+
+TK = 64
+D = 128
+WW = 2 * D
+
+SCRATCH = {
+    "xown": ("sbuf", [D, TK], "bfloat16"),
+    "xd": ("dram", [D, TK], "bfloat16"),
+    "xdrel": ("dram", [D, TK], "bfloat16"),
+    "xin1": ("sbuf", [D, TK], "bfloat16"),
+    "xin2": ("sbuf", [D, TK], "bfloat16"),
+    "wall": ("sbuf", [D, 4 * WW], "bfloat16"),
+    "gO": ("sbuf", [D, 4 * TK], "bfloat16"),
+    "gX1": ("sbuf", [D, 4 * TK], "bfloat16"),
+    "gX2": ("sbuf", [D, 4 * TK], "bfloat16"),
+    "rX1": ("sbuf", [D, TK], "bfloat16"),
+    "rX2": ("sbuf", [D, TK], "bfloat16"),
+    "land": ("sbuf", [D, TK], "bfloat16"),
+    "yout": ("sbuf", [D, TK], "bfloat16"),
+    "hO1": ("psum", [D, 512], "float32"),
+    "hO2": ("psum", [D, 512], "float32"),
+    "yO": ("psum", [D, 512], "float32"),
+    "hX1": ("psum", [D, 512], "float32"),
+    "yX1": ("psum", [D, 512], "float32"),
+    "hX2": ("psum", [D, 512], "float32"),
+    "yX2": ("psum", [D, 512], "float32"),
+}
+SEMAPHORES = ["ldx", "ldxd", "ldw", "xrel", "x1", "x2", "ws1", "ws2", "ws3", "res", "sent",
+              "tO1", "aO1", "tO2", "aO2", "mO",
+              "tX1", "aX1", "mX1", "cX1", "tX2", "aX2", "mX2", "cX2", "vy", "sty"]
+
+
+def _count(mask):
+    return bin(mask).count("1")
+
+
+def _lowest(mask, n):
+    out, got, i = 0, 0, 0
+    while got < n:
+        if (mask >> i) & 1:
+            out |= 1 << i
+            got += 1
+        i += 1
+    return out
+
+
+def _plan(cores, topo):
+    chips = []
+    for c in cores:
+        if topo.chip(c) not in chips:
+            chips.append(topo.chip(c))
+    plane_a = [chips[0]] + [ch for ch in chips[1:] if topo.same_plane(chips[0], ch)]
+    plane_b = [ch for ch in chips if ch not in plane_a]
+    plan = {}
+    for mine, other in ((plane_a, plane_b), (plane_b, plane_a)):
+        for i, ch in enumerate(mine):
+            members = [c for c in cores if topo.chip(c) == ch]
+            over = [c for c in cores if topo.chip(c) in other]
+            port = [c for c in members if all(topo.may_write(c, d) for d in over)][0]
+            plain = [c for c in members if c != port][0]
+            plan[ch] = (plain, port, mine[1 - i], other[i])
+    return plan
+
+
+def rank_program(g, core, T, topo):
+    if T.rank_of(core) is None:
+        return
+    S = T.sem
+    te, ve, ac, sy = g.tensor, g.vector, g.scalar, g.sync
+    gelu = ActivationFunctionType.Gelu_apprx_tanh
+
+    plan = _plan(T.cores, topo)
+    plain, port, far, cross = plan[topo.chip(core)]
+    is_port = core == port
+    partner = plain if is_port else port
+    far_plain, far_port = plan[far][0], plan[far][1]
+    cross_plain, cross_port = plan[cross][0], plan[cross][1]
+
+    m_off = topo.mask(core, far_port)
+    m_on = topo.mask(core, partner) & ~m_off
+    m_rel = _lowest(m_on, 4)
+    n_off, n_on, n_rel = _count(m_off), _count(m_on), _count(m_rel)
+
+    def w1(s):
+        return T.wall[:, s * WW:s * WW + D]
+
+    def w2(s):
+        return T.wall[:, s * WW + D:(s + 1) * WW]
+
+    def slot(s):
+        return T.wall[:, s * WW:(s + 1) * WW]
+
+    def blk(t, s):
+        return t[:, s * TK:(s + 1) * TK]
+
+    sent = [0]
+
+    def send(dst, out_ap, in_ap, sem, mask):
+        rid, pid, _se = topo.addr(dst)
+        g.remote_dma(out_ap=out_ap, in_ap=in_ap, remote_sem=sem, local_sem=S.sent, pid=pid, routing_id=rid,
+                     dma_engine_mask=mask)
+        sent[0] += _count(mask)
+
+    def send_fused(items):
+        trs = []
+        for dst, out_ap, in_ap, sem, mask in items:
+            rid, pid, _se = topo.addr(dst)
+            trs.append(RemoteDMATransfer(dst_ids=[DstId(rid=rid, pnc=pid)], dma_engine_mask=mask, remote_sem=sem,
+                                         src=in_ap, dst=out_ap))
+            sent[0] += _count(mask)
+        g.remote_dma_fused(trs, local_sem=S.sent)
+
+    if is_port:
+        sy.dma_start(T.xown[:], T.x[:]).then_inc(S.ldx, 16)
+        ac.dma_start(w1(0), T.w1[:]).then_inc(S.ldw, 16)
+        sy.dma_start(w2(0), T.w2[:]).then_inc(S.ldw, 16)
+    else:
+        sy.dma_start(T.xd[:], T.x[:]).then_inc(S.ldxd, 16)
+        ac.dma_start(w1(0), T.w1[:]).then_inc(S.ldw, 16)
+        sy.dma_start(w2(0), T.w2[:]).then_inc(S.ldw, 16)
+        ac.dma_start(T.xown[:], T.x[:]).then_inc(S.ldx, 16)
+
+    if is_port:
+        g.wait_ge(S.ldx, 16)
+        send(cross_port, T.xin1[:], T.xown[:], S.x1, m_off)
+        g.wait_ge(S.ldw, 32)
+        send(far_port, slot(3), slot(0), S.ws3, m_off)
+        g.wait_ge(S.xrel, n_rel)
+        send(cross_port, T.xin2[:], T.xdrel[:], S.x2, m_off)
+        send_fused([(far_plain, slot(3), slot(0), S.ws3, m_off),
+                    (partner, slot(1), slot(0), S.ws1, m_on)])
+    else:
+        g.wait_ge(S.ldxd, 16)
+        send(partner, T.xdrel[:], T.xd[:], S.xrel, m_rel)
+        g.wait_ge(S.ldw, 32)
+        send_fused([(far_port, slot(2), slot(0), S.ws2, m_off),
+                    (partner, slot(1), slot(0), S.ws1, m_on)])
+        send(far_plain, slot(2), slot(0), S.ws2, m_off)
+
+    te.wait_ge(S.ldx, 16)
+    te.wait_ge(S.ldw, 32)
+    te.matmul(blk(T.hO1, 0), w1(0), T.xown[:], True, True).then_inc(S.tO1, 1)
+    ac.wait_ge(S.tO1, 1)
+    ac.activation(blk(T.gO, 0), blk(T.hO1, 0), gelu).then_inc(S.aO1, 1)
+    te.wait_ge(S.aO1, 1)
+    te.matmul(blk(T.yO, 0), w2(0), blk(T.gO, 0), True, False).then_inc(S.mO, 1)
+
+    te.wait_ge(S.ws1, n_on)
+    te.wait_ge(S.ws2, n_off)
+    te.wait_ge(S.ws3, n_off)
+
+    if is_port:
+        streams = ((T.xin1, S.x1, T.hX1, T.gX1, T.yX1, T.rX1, S.tX1, S.aX1, S.mX1, S.cX1, cross_port),
+                   (T.xin2, S.x2, T.hX2, T.gX2, T.yX2, T.rX2, S.tX2, S.aX2, S.mX2, S.cX2, cross_plain))
+        for xin, sx, h, gl, yp, r, st, sa, sm, sc, owner in streams:
+            te.wait_ge(sx, n_off)
+            for s in range(4):
+                te.matmul(blk(h, s), w1(s), xin[:], True, True).then_inc(st, 1)
+            ac.wait_ge(st, 4)
+            ac.activation(gl[:], h[:, 0:4 * TK], gelu).then_inc(sa, 1)
+            te.wait_ge(sa, 1)
+            for s in range(4):
+                te.matmul(blk(yp, 0), w2(s), blk(gl, s), s == 0, s == 3).then_inc(sm, 1)
+            ve.wait_ge(sm, 4)
+            ve.tensor_copy(r[:], blk(yp, 0)).then_inc(sc, 1)
+            g.wait_ge(sc, 1)
+            send(owner, T.land[:], r[:], S.res, m_off)
+
+    for s in range(1, 4):
+        te.matmul(blk(T.hO2, s - 1), w1(s), T.xown[:], True, True).then_inc(S.tO2, 1)
+    ac.wait_ge(S.tO2, 3)
+    ac.activation(T.gO[:, TK:4 * TK], T.hO2[:, 0:3 * TK], gelu).then_inc(S.aO2, 1)
+    te.wait_ge(S.aO2, 1)
+    for s in range(1, 4):
+        te.matmul(blk(T.yO, 0), w2(s), blk(T.gO, s), False, s == 3).then_inc(S.mO, 1)
+
+    ve.wait_ge(S.mO, 4)
+    ve.wait_ge(S.res, n_off)
+    ve.tensor_tensor(T.yout[:], blk(T.yO, 0), T.land[:], AluOpType.add).then_inc(S.vy, 1)
+    sy.wait_ge(S.vy, 1)
+    sy.dma_start(T.y[:], T.yout[:]).then_inc(S.sty, 16)
+    sy.wait_ge(S.sty, 16)
+
+    g.wait_ge(S.sent, sent[0])

@@ -24,12 +24,13 @@ SCRATCH = {
     "yO": ("psum", [D, 512], "float32"),
     "hX1": ("psum", [D, 512], "float32"),
     "yX1": ("psum", [D, 512], "float32"),
-    "hX2": ("psum", [D, 512], "float32"),
+    "hA": ("psum", [D, 512], "float32"),
+    "hB": ("psum", [D, 512], "float32"),
     "yX2": ("psum", [D, 512], "float32"),
 }
-SEMAPHORES = ["ldx", "ldxd", "ldw", "xrel", "x1", "x2", "ws1", "ws2", "ws3", "res", "sent",
+SEMAPHORES = ["ldx", "ldxd", "ldw1", "ldw2", "xrel", "x1", "x2", "wa", "wb", "wb3", "ws1", "ws2", "ws3", "res", "sent",
               "tO1", "aO1", "tO2", "aO2", "mO",
-              "tX1", "aX1", "mX1", "cX1", "tX2", "aX2", "mX2", "cX2", "vy", "sty"]
+              "tX1", "aX1", "mX1", "cX1", "tA", "tB", "aA", "aB", "mX2", "cX2", "vy", "sty"]
 
 
 def _count(mask):
@@ -112,69 +113,103 @@ def rank_program(g, core, T, topo):
             sent[0] += _count(mask)
         g.remote_dma_fused(trs, local_sem=S.sent)
 
-    if is_port:
-        sy.dma_start(T.xown[:], T.x[:]).then_inc(S.ldx, 16)
-        ac.dma_start(w1(0), T.w1[:]).then_inc(S.ldw, 16)
-        sy.dma_start(w2(0), T.w2[:]).then_inc(S.ldw, 16)
-    else:
-        sy.dma_start(T.xd[:], T.x[:]).then_inc(S.ldxd, 16)
-        ac.dma_start(w1(0), T.w1[:]).then_inc(S.ldw, 16)
-        sy.dma_start(w2(0), T.w2[:]).then_inc(S.ldw, 16)
-        ac.dma_start(T.xown[:], T.x[:]).then_inc(S.ldx, 16)
+    sy.dma_start(T.xd[:], T.x[:]).then_inc(S.ldxd, 16)
+    ac.dma_start(w1(0), T.w1[:]).then_inc(S.ldw1, 16)
+    sy.dma_start(w2(0), T.w2[:]).then_inc(S.ldw2, 16)
+    ac.dma_start(T.xown[:], T.x[:]).then_inc(S.ldx, 16)
 
+    g.wait_ge(S.ldxd, 16)
     if is_port:
-        g.wait_ge(S.ldx, 16)
-        send(cross_port, T.xin1[:], T.xown[:], S.x1, m_off)
-        g.wait_ge(S.ldw, 32)
-        send(far_port, slot(3), slot(0), S.ws3, m_off)
+        send(cross_port, T.xin1[:], T.xd[:], S.x1, m_off)
+        g.wait_ge(S.ldw1, 16)
+        send(far_port, w1(3), w1(0), S.wa, m_off)
         g.wait_ge(S.xrel, n_rel)
         send(cross_port, T.xin2[:], T.xdrel[:], S.x2, m_off)
+        g.wait_ge(S.ldw2, 16)
+        send(far_port, w2(3), w2(0), S.wb3, m_off)
         send_fused([(far_plain, slot(3), slot(0), S.ws3, m_off),
                     (partner, slot(1), slot(0), S.ws1, m_on)])
     else:
-        g.wait_ge(S.ldxd, 16)
         send(partner, T.xdrel[:], T.xd[:], S.xrel, m_rel)
-        g.wait_ge(S.ldw, 32)
-        send_fused([(far_port, slot(2), slot(0), S.ws2, m_off),
-                    (partner, slot(1), slot(0), S.ws1, m_on)])
+        g.wait_ge(S.ldw1, 16)
+        send_fused([(far_port, w1(2), w1(0), S.wa, m_off),
+                    (partner, w1(1), w1(0), S.wa, m_on)])
+        g.wait_ge(S.ldw2, 16)
+        send_fused([(far_port, w2(2), w2(0), S.wb, m_off),
+                    (partner, w2(1), w2(0), S.wb, m_on)])
         send(far_plain, slot(2), slot(0), S.ws2, m_off)
 
     te.wait_ge(S.ldx, 16)
-    te.wait_ge(S.ldw, 32)
+    te.wait_ge(S.ldw1, 16)
     te.matmul(blk(T.hO1, 0), w1(0), T.xown[:], True, True).then_inc(S.tO1, 1)
     ac.wait_ge(S.tO1, 1)
     ac.activation(blk(T.gO, 0), blk(T.hO1, 0), gelu).then_inc(S.aO1, 1)
     te.wait_ge(S.aO1, 1)
+    te.wait_ge(S.ldw2, 16)
     te.matmul(blk(T.yO, 0), w2(0), blk(T.gO, 0), True, False).then_inc(S.mO, 1)
 
-    te.wait_ge(S.ws1, n_on)
-    te.wait_ge(S.ws2, n_off)
-    te.wait_ge(S.ws3, n_off)
-
     if is_port:
-        streams = ((T.xin1, S.x1, T.hX1, T.gX1, T.yX1, T.rX1, S.tX1, S.aX1, S.mX1, S.cX1, cross_port),
-                   (T.xin2, S.x2, T.hX2, T.gX2, T.yX2, T.rX2, S.tX2, S.aX2, S.mX2, S.cX2, cross_plain))
-        for xin, sx, h, gl, yp, r, st, sa, sm, sc, owner in streams:
-            te.wait_ge(sx, n_off)
-            for s in range(4):
-                te.matmul(blk(h, s), w1(s), xin[:], True, True).then_inc(st, 1)
-            ac.wait_ge(st, 4)
-            ac.activation(gl[:], h[:, 0:4 * TK], gelu).then_inc(sa, 1)
-            te.wait_ge(sa, 1)
-            for s in range(4):
-                te.matmul(blk(yp, 0), w2(s), blk(gl, s), s == 0, s == 3).then_inc(sm, 1)
-            ve.wait_ge(sm, 4)
-            ve.tensor_copy(r[:], blk(yp, 0)).then_inc(sc, 1)
-            g.wait_ge(sc, 1)
-            send(owner, T.land[:], r[:], S.res, m_off)
+        te.wait_ge(S.wa, n_on + 2 * n_off)
+        te.wait_ge(S.x1, n_off)
+        for s in range(4):
+            te.matmul(blk(T.hX1, s), w1(s), T.xin1[:], True, True).then_inc(S.tX1, 1)
+        for s in range(1, 4):
+            te.matmul(blk(T.hO2, s - 1), w1(s), T.xown[:], True, True).then_inc(S.tO2, 1)
+        ac.wait_ge(S.tX1, 4)
+        ac.activation(T.gX1[:], T.hX1[:, 0:4 * TK], gelu).then_inc(S.aX1, 1)
 
-    for s in range(1, 4):
-        te.matmul(blk(T.hO2, s - 1), w1(s), T.xown[:], True, True).then_inc(S.tO2, 1)
-    ac.wait_ge(S.tO2, 3)
-    ac.activation(T.gO[:, TK:4 * TK], T.hO2[:, 0:3 * TK], gelu).then_inc(S.aO2, 1)
-    te.wait_ge(S.aO2, 1)
-    for s in range(1, 4):
-        te.matmul(blk(T.yO, 0), w2(s), blk(T.gO, s), False, s == 3).then_inc(S.mO, 1)
+        te.wait_ge(S.x2, n_off)
+        for s in range(2):
+            te.matmul(blk(T.hA, s), w1(s), T.xin2[:], True, True).then_inc(S.tA, 1)
+        for s in range(2):
+            te.matmul(blk(T.hB, s), w1(2 + s), T.xin2[:], True, True).then_inc(S.tB, 1)
+        ac.wait_ge(S.tA, 2)
+        ac.activation(T.gX2[:, 0:2 * TK], T.hA[:, 0:2 * TK], gelu).then_inc(S.aA, 1)
+        ac.wait_ge(S.tB, 2)
+        ac.activation(T.gX2[:, 2 * TK:4 * TK], T.hB[:, 0:2 * TK], gelu).then_inc(S.aB, 1)
+
+        te.wait_ge(S.aX1, 1)
+        te.wait_ge(S.wb, n_on + n_off)
+        for s in range(3):
+            te.matmul(blk(T.yX1, 0), w2(s), blk(T.gX1, s), s == 0, False).then_inc(S.mX1, 1)
+        te.wait_ge(S.aA, 1)
+        for s in range(2):
+            te.matmul(blk(T.yX2, 0), w2(s), blk(T.gX2, s), s == 0, False).then_inc(S.mX2, 1)
+        te.wait_ge(S.aB, 1)
+        te.matmul(blk(T.yX2, 0), w2(2), blk(T.gX2, 2), False, False).then_inc(S.mX2, 1)
+        te.wait_ge(S.wb3, n_off)
+        te.matmul(blk(T.yX1, 0), w2(3), blk(T.gX1, 3), False, True).then_inc(S.mX1, 1)
+        te.matmul(blk(T.yX2, 0), w2(3), blk(T.gX2, 3), False, True).then_inc(S.mX2, 1)
+        ve.wait_ge(S.mX1, 4)
+        ve.tensor_copy(T.rX1[:], blk(T.yX1, 0)).then_inc(S.cX1, 1)
+        g.wait_ge(S.cX1, 1)
+        send(cross_port, T.land[:], T.rX1[:], S.res, m_off)
+        ve.wait_ge(S.mX2, 4)
+        ve.tensor_copy(T.rX2[:], blk(T.yX2, 0)).then_inc(S.cX2, 1)
+        g.wait_ge(S.cX2, 1)
+        send(cross_plain, T.land[:], T.rX2[:], S.res, m_off)
+
+        ac.wait_ge(S.tO2, 3)
+        ac.activation(T.gO[:, TK:4 * TK], T.hO2[:, 0:3 * TK], gelu).then_inc(S.aO2, 1)
+        te.wait_ge(S.aO2, 1)
+        for s in range(1, 4):
+            te.matmul(blk(T.yO, 0), w2(s), blk(T.gO, s), False, s == 3).then_inc(S.mO, 1)
+    else:
+        te.wait_ge(S.ws2, n_off)
+        te.matmul(blk(T.hO2, 0), w1(2), T.xown[:], True, True).then_inc(S.tO2, 1)
+        ac.wait_ge(S.tO2, 1)
+        ac.activation(blk(T.gO, 2), blk(T.hO2, 0), gelu).then_inc(S.aO2, 1)
+        te.wait_ge(S.aO2, 1)
+        te.matmul(blk(T.yO, 0), w2(2), blk(T.gO, 2), False, False).then_inc(S.mO, 1)
+        te.wait_ge(S.ws1, n_on)
+        te.wait_ge(S.ws3, n_off)
+        te.matmul(blk(T.hX1, 0), w1(1), T.xown[:], True, True).then_inc(S.tX1, 1)
+        te.matmul(blk(T.hX1, 1), w1(3), T.xown[:], True, True).then_inc(S.tX1, 1)
+        ac.wait_ge(S.tX1, 2)
+        ac.activation(T.gX1[:, 0:2 * TK], T.hX1[:, 0:2 * TK], gelu).then_inc(S.aX1, 1)
+        te.wait_ge(S.aX1, 1)
+        te.matmul(blk(T.yO, 0), w2(1), blk(T.gX1, 0), False, False).then_inc(S.mO, 1)
+        te.matmul(blk(T.yO, 0), w2(3), blk(T.gX1, 1), False, True).then_inc(S.mO, 1)
 
     ve.wait_ge(S.mO, 4)
     ve.wait_ge(S.res, n_off)

from concourse.bass import DstId, RemoteDMATransfer
from concourse.mybir import AluOpType, ActivationFunctionType

TK = 64
D = 128
WW = 2 * D

SCRATCH = {
    "xown": ("sbuf", [D, TK], "bfloat16"),
    "xd": ("dram", [D, TK], "bfloat16"),
    "xdrel": ("dram", [D, TK], "bfloat16"),
    "xin1": ("sbuf", [D, TK], "bfloat16"),
    "xin2": ("sbuf", [D, TK], "bfloat16"),
    "wall": ("sbuf", [D, 4 * WW], "bfloat16"),
    "gO": ("sbuf", [D, 4 * TK], "bfloat16"),
    "gX1": ("sbuf", [D, 4 * TK], "bfloat16"),
    "gX2": ("sbuf", [D, 4 * TK], "bfloat16"),
    "rX1": ("sbuf", [D, TK], "bfloat16"),
    "rX2": ("sbuf", [D, TK], "bfloat16"),
    "land": ("sbuf", [D, TK], "bfloat16"),
    "yout": ("sbuf", [D, TK], "bfloat16"),
    "hO1": ("psum", [D, 512], "float32"),
    "hO2": ("psum", [D, 512], "float32"),
    "yO": ("psum", [D, 512], "float32"),
    "hX1": ("psum", [D, 512], "float32"),
    "yX1": ("psum", [D, 512], "float32"),
    "hA": ("psum", [D, 512], "float32"),
    "hB": ("psum", [D, 512], "float32"),
    "yX2": ("psum", [D, 512], "float32"),
}
SEMAPHORES = ["ldx", "ldxd", "ldw1", "ldw2", "xrel", "x1", "x2", "wa", "wb", "wb3", "ws1", "ws2", "ws3", "res", "sent",
              "tO1", "aO1", "tO2", "aO2", "mO",
              "tX1", "aX1", "mX1", "cX1", "tA", "tB", "aA", "aB", "mX2", "cX2", "vy", "sty"]


def _count(mask):
    return bin(mask).count("1")


def _lowest(mask, n):
    out, got, i = 0, 0, 0
    while got < n:
        if (mask >> i) & 1:
            out |= 1 << i
            got += 1
        i += 1
    return out


def _plan(cores, topo):
    chips = []
    for c in cores:
        if topo.chip(c) not in chips:
            chips.append(topo.chip(c))
    plane_a = [chips[0]] + [ch for ch in chips[1:] if topo.same_plane(chips[0], ch)]
    plane_b = [ch for ch in chips if ch not in plane_a]
    plan = {}
    for mine, other in ((plane_a, plane_b), (plane_b, plane_a)):
        for i, ch in enumerate(mine):
            members = [c for c in cores if topo.chip(c) == ch]
            over = [c for c in cores if topo.chip(c) in other]
            port = [c for c in members if all(topo.may_write(c, d) for d in over)][0]
            plain = [c for c in members if c != port][0]
            plan[ch] = (plain, port, mine[1 - i], other[i])
    return plan


def rank_program(g, core, T, topo):
    if T.rank_of(core) is None:
        return
    S = T.sem
    te, ve, ac, sy = g.tensor, g.vector, g.scalar, g.sync
    gelu = ActivationFunctionType.Gelu_apprx_tanh

    plan = _plan(T.cores, topo)
    plain, port, far, cross = plan[topo.chip(core)]
    is_port = core == port
    partner = plain if is_port else port
    far_plain, far_port = plan[far][0], plan[far][1]
    cross_plain, cross_port = plan[cross][0], plan[cross][1]

    m_off = topo.mask(core, far_port)
    m_on = topo.mask(core, partner) & ~m_off
    m_rel = _lowest(m_on, 4)
    n_off, n_on, n_rel = _count(m_off), _count(m_on), _count(m_rel)

    def w1(s):
        return T.wall[:, s * WW:s * WW + D]

    def w2(s):
        return T.wall[:, s * WW + D:(s + 1) * WW]

    def slot(s):
        return T.wall[:, s * WW:(s + 1) * WW]

    def blk(t, s):
        return t[:, s * TK:(s + 1) * TK]

    sent = [0]

    def send(dst, out_ap, in_ap, sem, mask):
        rid, pid, _se = topo.addr(dst)
        g.remote_dma(out_ap=out_ap, in_ap=in_ap, remote_sem=sem, local_sem=S.sent, pid=pid, routing_id=rid,
                     dma_engine_mask=mask)
        sent[0] += _count(mask)

    def send_fused(items):
        trs = []
        for dst, out_ap, in_ap, sem, mask in items:
            rid, pid, _se = topo.addr(dst)
            trs.append(RemoteDMATransfer(dst_ids=[DstId(rid=rid, pnc=pid)], dma_engine_mask=mask, remote_sem=sem,
                                         src=in_ap, dst=out_ap))
            sent[0] += _count(mask)
        g.remote_dma_fused(trs, local_sem=S.sent)

    sy.dma_start(T.xd[:], T.x[:]).then_inc(S.ldxd, 16)
    ac.dma_start(w1(0), T.w1[:]).then_inc(S.ldw1, 16)
    sy.dma_start(w2(0), T.w2[:]).then_inc(S.ldw2, 16)
    ac.dma_start(T.xown[:], T.x[:]).then_inc(S.ldx, 16)

    g.wait_ge(S.ldxd, 16)
    if is_port:
        send(cross_port, T.xin1[:], T.xd[:], S.x1, m_off)
        g.wait_ge(S.ldw1, 16)
        send(far_port, w1(3), w1(0), S.wa, m_off)
        g.wait_ge(S.xrel, n_rel)
        send(cross_port, T.xin2[:], T.xdrel[:], S.x2, m_off)
        g.wait_ge(S.ldw2, 16)
        send(far_port, w2(3), w2(0), S.wb3, m_off)
        send_fused([(far_plain, slot(3), slot(0), S.ws3, m_off),
                    (partner, slot(1), slot(0), S.ws1, m_on)])
    else:
        send(partner, T.xdrel[:], T.xd[:], S.xrel, m_rel)
        g.wait_ge(S.ldw1, 16)
        send_fused([(far_port, w1(2), w1(0), S.wa, m_off),
                    (partner, w1(1), w1(0), S.wa, m_on)])
        g.wait_ge(S.ldw2, 16)
        send_fused([(far_port, w2(2), w2(0), S.wb, m_off),
                    (partner, w2(1), w2(0), S.wb, m_on)])
        send(far_plain, slot(2), slot(0), S.ws2, m_off)

    te.wait_ge(S.ldx, 16)
    te.wait_ge(S.ldw1, 16)
    te.matmul(blk(T.hO1, 0), w1(0), T.xown[:], True, True).then_inc(S.tO1, 1)
    ac.wait_ge(S.tO1, 1)
    ac.activation(blk(T.gO, 0), blk(T.hO1, 0), gelu).then_inc(S.aO1, 1)
    te.wait_ge(S.aO1, 1)
    te.wait_ge(S.ldw2, 16)
    te.matmul(blk(T.yO, 0), w2(0), blk(T.gO, 0), True, False).then_inc(S.mO, 1)

    if is_port:
        te.wait_ge(S.wa, n_on + 2 * n_off)
        te.wait_ge(S.x1, n_off)
        for s in range(4):
            te.matmul(blk(T.hX1, s), w1(s), T.xin1[:], True, True).then_inc(S.tX1, 1)
        for s in range(1, 4):
            te.matmul(blk(T.hO2, s - 1), w1(s), T.xown[:], True, True).then_inc(S.tO2, 1)
        ac.wait_ge(S.tX1, 4)
        ac.activation(T.gX1[:], T.hX1[:, 0:4 * TK], gelu).then_inc(S.aX1, 1)

        te.wait_ge(S.x2, n_off)
        for s in range(2):
            te.matmul(blk(T.hA, s), w1(s), T.xin2[:], True, True).then_inc(S.tA, 1)
        for s in range(2):
            te.matmul(blk(T.hB, s), w1(2 + s), T.xin2[:], True, True).then_inc(S.tB, 1)
        ac.wait_ge(S.tA, 2)
        ac.activation(T.gX2[:, 0:2 * TK], T.hA[:, 0:2 * TK], gelu).then_inc(S.aA, 1)
        ac.wait_ge(S.tB, 2)
        ac.activation(T.gX2[:, 2 * TK:4 * TK], T.hB[:, 0:2 * TK], gelu).then_inc(S.aB, 1)

        te.wait_ge(S.aX1, 1)
        te.wait_ge(S.wb, n_on + n_off)
        for s in range(3):
            te.matmul(blk(T.yX1, 0), w2(s), blk(T.gX1, s), s == 0, False).then_inc(S.mX1, 1)
        te.wait_ge(S.aA, 1)
        for s in range(2):
            te.matmul(blk(T.yX2, 0), w2(s), blk(T.gX2, s), s == 0, False).then_inc(S.mX2, 1)
        te.wait_ge(S.aB, 1)
        te.matmul(blk(T.yX2, 0), w2(2), blk(T.gX2, 2), False, False).then_inc(S.mX2, 1)
        te.wait_ge(S.wb3, n_off)
        te.matmul(blk(T.yX1, 0), w2(3), blk(T.gX1, 3), False, True).then_inc(S.mX1, 1)
        te.matmul(blk(T.yX2, 0), w2(3), blk(T.gX2, 3), False, True).then_inc(S.mX2, 1)
        ve.wait_ge(S.mX1, 4)
        ve.tensor_copy(T.rX1[:], blk(T.yX1, 0)).then_inc(S.cX1, 1)
        g.wait_ge(S.cX1, 1)
        send(cross_port, T.land[:], T.rX1[:], S.res, m_off)
        ve.wait_ge(S.mX2, 4)
        ve.tensor_copy(T.rX2[:], blk(T.yX2, 0)).then_inc(S.cX2, 1)
        g.wait_ge(S.cX2, 1)
        send(cross_plain, T.land[:], T.rX2[:], S.res, m_off)

        ac.wait_ge(S.tO2, 3)
        ac.activation(T.gO[:, TK:4 * TK], T.hO2[:, 0:3 * TK], gelu).then_inc(S.aO2, 1)
        te.wait_ge(S.aO2, 1)
        for s in range(1, 4):
            te.matmul(blk(T.yO, 0), w2(s), blk(T.gO, s), False, s == 3).then_inc(S.mO, 1)
    else:
        te.wait_ge(S.ws2, n_off)
        te.matmul(blk(T.hO2, 0), w1(2), T.xown[:], True, True).then_inc(S.tO2, 1)
        ac.wait_ge(S.tO2, 1)
        ac.activation(blk(T.gO, 2), blk(T.hO2, 0), gelu).then_inc(S.aO2, 1)
        te.wait_ge(S.aO2, 1)
        te.matmul(blk(T.yO, 0), w2(2), blk(T.gO, 2), False, False).then_inc(S.mO, 1)
        te.wait_ge(S.ws1, n_on)
        te.wait_ge(S.ws3, n_off)
        te.matmul(blk(T.hX1, 0), w1(1), T.xown[:], True, True).then_inc(S.tX1, 1)
        te.matmul(blk(T.hX1, 1), w1(3), T.xown[:], True, True).then_inc(S.tX1, 1)
        ac.wait_ge(S.tX1, 2)
        ac.activation(T.gX1[:, 0:2 * TK], T.hX1[:, 0:2 * TK], gelu).then_inc(S.aX1, 1)
        te.wait_ge(S.aX1, 1)
        te.matmul(blk(T.yO, 0), w2(1), blk(T.gX1, 0), False, False).then_inc(S.mO, 1)
        te.matmul(blk(T.yO, 0), w2(3), blk(T.gX1, 1), False, True).then_inc(S.mO, 1)

    ve.wait_ge(S.mO, 4)
    ve.wait_ge(S.res, n_off)
    ve.tensor_tensor(T.yout[:], blk(T.yO, 0), T.land[:], AluOpType.add).then_inc(S.vy, 1)
    sy.wait_ge(S.vy, 1)
    sy.dma_start(T.y[:], T.yout[:]).then_inc(S.sty, 16)
    sy.wait_ge(S.sty, 16)

    g.wait_ge(S.sent, sent[0])
